import numpy as np, ml_dtypes
CORES = [83,85,87,115,117,119]
N = 6
BF = ml_dtypes.bfloat16
def gentries(a):
    return np.ascontiguousarray(a.reshape(8, 16, -1).transpose(0, 2, 1)).reshape(8, -1)
def gtable(e):
    e = np.asarray(e); return np.ascontiguousarray(e.reshape(8, -1, 16).transpose(0, 2, 1)).reshape(128, -1).astype(np.int32)
W, n, V, C, Z = 5, 2048, 16384, 512, 128
def counts(rng, h, z):
    c = np.zeros((N, 8, W), np.int64)
    for r in range(N):
        for g in range(8):
            m = int(h[r, g] - z[r, g]) - (W - 2); b = np.sort(rng.integers(0, m + 1, W - 3))
            c[r, g, 0] = n - h[r, g]; c[r, g, 1:W - 1] = np.diff(np.concatenate([[0], b, [m]])) + 1; c[r, g, W - 1] = z[r, g]
    return c
def some(rng):
    return rng.integers(C - C // 4, C + 1, (N, 8)), rng.integers(Z // 2, Z + 1, (N, 8))
def names(rng):
    return np.stack([np.stack([rng.permutation(V)[:n] for g in range(8)]) for r in range(N)]).astype(np.int64)
def depths(rng, c):
    return np.stack([np.stack([rng.permutation(np.repeat(np.arange(W), c[r, g])) for g in range(8)]) for r in range(N)])
def link(rng, o, dep):
    x = np.zeros((N, 8, n), np.int64)
    for r in range(N):
        q = (r + 1) % N
        for g in range(8):
            m = np.ones(V, bool); m[o[q, g]] = False; free = np.flatnonzero(m)
            v = free[rng.integers(0, len(free), n)]
            for k in range(1, W):
                i = np.flatnonzero(dep[r, g] == k)
                if len(i):
                    t = np.flatnonzero(dep[q, g] == k - 1 if k < W - 1 else dep[q, g] >= W - 2)
                    v[i] = o[q, g][t[rng.integers(0, len(t), len(i))]]
            x[r, g] = v
    return x
def pack(o, x, s):
    return {"own": np.stack([gtable(a) for a in o]), "nxt": np.stack([gtable(a) for a in x]), "pts": np.asarray(s).astype(np.int32)}
def points(rng):
    return rng.integers(0, 256, (N, 8, n))
def setup_inputs(rng):
    h, z = some(rng); o = names(rng); dep = depths(rng, counts(rng, h, z))
    return pack(o, link(rng, o, dep), points(rng))
def setup_inputs_full(rng):
    o = names(rng); c = counts(rng, np.full((N, 8), C), np.full((N, 8), Z)); e = rng.permutation(8)[:4]
    c[:, e, 1:W - 2] = 1; c[:, e, W - 2] = C - Z - (W - 3)
    dep = depths(rng, c)
    return pack(o, link(rng, o, dep), points(rng))
def setup_inputs_few(rng):
    h, z = some(rng); e = rng.permutation(8); q = int(rng.integers(0, N)); o = names(rng)
    z[:, e[2]] = 1; z[:, e[3]] = np.where(rng.random(N) < 0.5, 0, z[:, e[3]]); z[q, e[3]] = 0; z[:, e[4]] = Z; h[:, e[4]] = C
    c = counts(rng, h, z); c[:, e[0], 0] = n; c[:, e[0], 1:] = 0
    for t in range(W - 1):
        r = (q - t) % N; c[r, e[1], 0] += np.sum(c[r, e[1], t + 1:]); c[r, e[1], t + 1:] = 0
    dep = depths(rng, c)
    return pack(o, link(rng, o, dep), points(rng))
def setup_inputs_repeats(rng):
    h, z = some(rng); o = names(rng); dep = depths(rng, counts(rng, h, z)); x = link(rng, o, dep)
    for r in range(N):
        for g in range(8):
            for k in (0, W - 1):
                i = np.flatnonzero(dep[r, g] == k); x[r, g, i] = x[r, g, i[0]]
    return pack(o, x, points(rng))
def setup_inputs_ends(rng):
    h, z = some(rng); dep = depths(rng, counts(rng, h, z))
    o = 1 + np.stack([np.stack([rng.permutation(V - 2)[:n] for g in range(8)]) for r in range(N)]).astype(np.int64)
    for r in range(N):
        for g in range(0, 8, 2):
            o[r, g, 0] = 0; o[r, g, n - 1] = V - 1; a = dep[r, g]
            i = np.flatnonzero(a == W - 1); j = i[rng.integers(0, len(i))]; u, v = int(a[0]), int(a[j]); a[j] = u; a[0] = v
            i = np.flatnonzero(a[1:] == W - 1) + 1; j = i[rng.integers(0, len(i))]; u, v = int(a[n - 1]), int(a[j]); a[j] = u; a[n - 1] = v
    x = link(rng, o, dep)
    x[:, 0::2, 0] = V - 1; x[:, 0::2, n - 1] = 0
    for g in range(1, 8, 2):
        m = (dep[:, g] == 0) & (rng.random((N, n)) < 0.5)
        x[:, g] = np.where(m, rng.integers(0, 2, (N, n)) * (V - 1), x[:, g])
    return pack(o, x, 255 * rng.integers(0, 2, (N, 8, n)))
def setup_inputs_spread(rng):
    z = np.maximum(Z >> rng.integers(0, 7, (N, 8)), 1); h = z + np.maximum((C - Z) >> rng.integers(0, 7, (N, 8)), W - 2)
    o = np.stack([np.stack([(rng.integers(0, V) + rng.permutation(n + n // 8)[:n]) % V for g in range(8)]) for r in range(N)]).astype(np.int64)
    o[:, 1::2] = np.sort(o[:, 1::2], axis=2)
    dep = depths(rng, counts(rng, h, z))
    return pack(o, link(rng, o, dep), 255 >> rng.integers(0, 9, (N, 8, n)))
def followers(o, x):
    to = np.zeros((N, 8, n), np.int64)
    for r in range(N):
        for g in range(8):
            where = np.full(V, -1, np.int64); where[o[(r + 1) % N, g]] = np.arange(n); to[r, g] = where[x[r, g]]
    return to
def step(p, v, t):
    return np.take_along_axis(np.roll(v, -t, axis=0), p, axis=2)
def chains(to, s):
    p = np.broadcast_to(np.arange(n), (N, 8, n)); tot = s.astype(np.int64)
    for t in range(1, W):
        p = np.where(p >= 0, step(np.maximum(p, 0), to, t - 1), -1)
        tot = tot + np.where(p >= 0, step(np.maximum(p, 0), s, t), 0)
    return p, tot
def check_inputs(d):
    try:
        o = np.stack([gentries(a) for a in d["own"]]).astype(np.int64); x = np.stack([gentries(a) for a in d["nxt"]]).astype(np.int64); s = np.asarray(d["pts"]).astype(np.int64)
        if o.shape != (N, 8, n) or x.shape != (N, 8, n) or s.shape != (N, 8, n): return ["shapes"]
        bad = []
        if s.min() < 0 or s.max() > 255: bad.append("points")
        if o.min() < 0 or o.max() >= V or x.min() < 0 or x.max() >= V: return bad + ["names in range"]
        if (np.diff(np.sort(o, axis=2), axis=2) == 0).any(): return bad + ["own names differ"]
        to = followers(o, x); p, tot = chains(to, s)
        if np.max(np.count_nonzero(to >= 0, axis=2)) > C: bad.append("followers")
        if np.max(np.count_nonzero(p >= 0, axis=2)) > Z: bad.append("kept")
        return bad
    except Exception:
        return ["shapes"]
def reference(own, nxt, pts):
    o = np.stack([gentries(a) for a in own]).astype(np.int64); x = np.stack([gentries(a) for a in nxt]).astype(np.int64)
    p, tot = chains(followers(o, x), pts)
    yk = np.full((N, 8, Z), -1, np.float32); ys = np.zeros((N, 8, Z), np.float32)
    for r in range(N):
        for g in range(8):
            i = np.flatnonzero(p[r, g] >= 0)
            yk[r, g, :len(i)] = o[r, g, i]; ys[r, g, :len(i)] = tot[r, g, i]
    return {"yk": yk, "ys": ys}

@@ -1,0 +1,357 @@
+from concourse.bass import DstId, RemoteDMATransfer
+from concourse.mybir import dt, AluOpType, AxisListType, ActivationFunctionType
+
+A = AluOpType
+F = ActivationFunctionType
+NV = 16384
+NE = 2048
+HE = NE // 2
+QE = NE // 4
+CH = 256
+BIG = 8192.0
+PF = 8.0
+NONE = 8 * CH + 8
+DW = NONE + 8
+CC = 512
+HC = CC // 2
+ZZ = 128
+SH = 16.0
+NA = 576
+NVEC = 6656
+NDMA = 4096
+NGP = 1024
+FW = 1024
+ROUND = 8388608.0
+
+
+def _bufs():
+    d = {}
+    for where, typ, items in (
+            ("sbuf", "int32", "owni:128 nxti:128 ptsi:128 pi:1 pm:1"),
+            ("sbuf", "uint16", "ou:128 nu:128 nr:128 fu:128 fl1:128 fl2:128 du:128 pu:32 ic:32 du2:32"),
+            ("sbuf", "bfloat16", "ptsb:128 xl1:128 p1:2048 w3:%d tab:16384 val:2048 gat:2048 lo:256 ipat:%d ca:%d cb:512 kk:512 ones:128"
+                                 " bd0:128 bd:128 tri:128 upp:128 za:144 zi:144 zk:144 vb:129 vb2:33" % (DW, NA, CC + NA)),
+            ("sbuf", "float32", "b2:%d b1:%d xx:%d ownf:128 ptf:128 tf:128 ilo:512 cwin:2560 rr:512 cw:512 owin:640"
+                                " zf:128 pmf:1 c0:1 c1:1 c2:1 c3:1 c1n:1 c2n:1 wc:1 wi:1 n1:1 i8:8 bcol:8 bco1:8 bcn:8 idf:128 onef:128"
+                                " ii:128 i512:128 i128:32 iv:128 ds:128 nv2:32 iv2:32 xs2:32 ds2:32 puf:32 icf:32 pur:32 icr:32" % (DW, DW, DW)),
+            ("dram", "bfloat16", "xo:128 xl2:128 xl3:128 xl4:128"),
+            ("psum", "float32", "psf0:512 psf1:512 psd:512 psw:512 psi:512 psk:512 pst:512")):
+        for it in items.split():
+            name, w = it.split(":")
+            d[name] = (where, [128, int(w)], typ)
+    return d
+
+
+SCRATCH = _bufs()
+EV = """ones tabg tab0 tabv tabs pi pm pmf c0 c1 c2 c3 cn n1 wc lo ilo i8 bcol bco1 bcn val onef bd0 bd tri upp idf zf z0 za zi zk ipat cap xxi
+ii i512 i128 w3t tails cpre vz opre ownf ptf tr tf ptsb nu ou scat ga gb fa fb fu vb nv iv dl xs ds du
+xc0 xc1 csa cs0 cs cb pw pq puf icf pu ic kk pk b2 b1 rr cw vb2 nv2 iv2 dl2 xs2 ds2 du2 osc""".split()
+SEMAPHORES = ["e_" + e for e in EV] + ["ldo", "ldn", "ldp", "dfl", "dvl", "din", "dxo", "dnp", "dx0", "dx1", "dr1", "dr2", "dr3", "dpt", "narr", "nsent",
+                                       "xa1", "xa2", "xa3", "xa4", "xsent", "fa1", "fa2", "fs1", "fs2", "qa1", "qa2", "qs1", "qs2", "out1", "out2"]
+
+
+def rank_program(g, core, T, topo):
+    rank = T.rank_of(core)
+    if rank is None:
+        return
+    n = len(T.cores)
+    V, S, P, Y = g.vector, g.scalar, g.tensor, g.sync
+    back = [T.cores[(rank - k) % n] for k in range(n)]
+    after = T.cores[(rank + 1) % n]
+
+    def sem(e):
+        return T.sem["e_" + e]
+
+    def done(ins, e):
+        ins.then_inc(sem(e), 1)
+
+    def wait(q, *es):
+        for e in es:
+            if isinstance(e, tuple):
+                q.wait_ge(sem(e[0]), e[1])
+            else:
+                q.wait_ge(sem(e), 1)
+
+    def const(buf, v, e):
+        done(g.iota(buf, [[0, buf.shape[1]]], int(v), 0, allow_small_or_imprecise_dtypes=True), e)
+
+    es = set(topo.engines(core, after))
+    for k in range(1, n - 1):
+        es &= set(topo.engines(core, back[k]))
+    E = sorted(es)[0:8]
+    M = sum(1 << e for e in E)
+    NEG = len(E)
+
+    def send(dst_ap, src_ap, dst, rs, ls):
+        rid, pid = topo.addr(dst)[:2]
+        g.remote_dma(dst_ap, src_ap, T.sem[rs], T.sem[ls], pid, rid, M)
+
+    def send_x(k1, k2):
+        tr = []
+        for k, half in ((k1, E[:NEG // 2]), (k2, E[NEG // 2:])):
+            rid, pid = topo.addr(back[k])[:2]
+            tr.append(RemoteDMATransfer(dst_ids=[DstId(rid=rid, pnc=pid)], dma_engine_mask=sum(1 << e for e in half), remote_sem=T.sem["xa%d" % k],
+                                        srcs=[T.xo[:]], dsts=[T["xl%d" % k][:]]))
+        g.remote_dma_fused(tr, local_sem=T.sem.xsent)
+
+    Y.dma_start(T.owni[:], T.own[:]).then_inc(T.sem.ldo, 16)
+    S.dma_start(T.nxti[:], T.nxt[:]).then_inc(T.sem.ldn, 16)
+    Y.dma_start(T.ptsi[:], T.pts[:]).then_inc(T.sem.ldp, 16)
+
+    done(g.iota(T.pi[:], [[0, 1]], 0, 1), "pi")
+    done(g.iota(T.i8[:], [[1, 8]], 0, 0, allow_small_or_imprecise_dtypes=True), "i8")
+    done(g.iota(T.lo[:], [[1, CH]], 0, 0, allow_small_or_imprecise_dtypes=True), "lo")
+    const(T.tab[:, NVEC + NDMA:NVEC + NDMA + NGP], -BIG, "tabg")
+    wait(g, "nu")
+    send(T.nr[:], T.nu[:], after, "narr", "nsent")
+    const(T.ones[:], 1, "ones")
+    wait(g, "ones")
+    done(g.affine_select(T.bd0[:], T.ones[:], [[-16, 8], [0, 16]], A.is_ge, 0.0, 0, 1), "bd0")
+    wait(g, "bd0")
+    done(g.affine_select(T.bd[:], T.bd0[:], [[16, 8], [0, 16]], A.is_ge, 0.0, 15, -1), "bd")
+    const(T.za[:], 0, "z0")
+    wait(g, "bd")
+    done(g.affine_select(T.tri[:], T.bd[:], [[1, 128]], A.is_gt, 0.0, 0, -1), "tri")
+    done(g.affine_select(T.upp[:], T.bd[:], [[-1, 128]], A.is_ge, 0.0, 0, 1), "upp")
+    done(g.iota(T.ii[:], [[16, 128]], CC, 0, allow_small_or_imprecise_dtypes=True), "ii")
+    const(T.zf[:], 0, "zf")
+    const(T.vb[:, 0:1], 0, "vz")
+    const(T.vb2[:, 0:1], 0, "vz")
+    done(g.iota(T.ilo[0:8, :], [[0, QE // CH], [1, CH]], int(SH), 0, allow_small_or_imprecise_dtypes=True), "ilo")
+    wait(g, "za")
+    const(T.zi[:], 0, "z0")
+    const(T.zk[:], 0, "z0")
+    const(T.w3[:, NE:DW], -BIG, "w3t")
+    g.wait_ge(T.sem.dxo, 16)
+    send_x(4, 3)
+    wait(g, ("fu", 2))
+    send(T.fl2[:], T.fu[:], back[3], "fa2", "fs2")
+    send(T.fl1[:], T.fu[:], back[2], "fa1", "fs1")
+    send_x(2, 1)
+    for b in ("b2", "b1"):
+        const(T[b][:, NE:DW], -BIG, "tails")
+    const(T.onef[:], 1, "onef")
+    wait(g, "onef")
+    done(g.affine_select(T.idf[:], T.onef[:], [[-1, 128]], A.is_equal, 0.0, 0, 1), "idf")
+    const(T.xx[:, 0:NA], 0, "xxi")
+    const(T.xx[:, NE:DW], 0, "xxi")
+    wait(g, "ptf")
+    g.wait_ge(T.sem.xa1, NEG // 2)
+    g.dma_start(T.ptf[:], T.xl1[:], accum_op=A.add).then_inc(T.sem.dpt, 16)
+    wait(g, "puf")
+    send(T.pur[:], T.puf[:], back[1], "qa1", "qs1")
+    wait(g, "icf")
+    send(T.icr[:], T.icf[:], back[1], "qa2", "qs2")
+
+    wait(Y, "tab0")
+    for a in range(NVEC, NVEC + NDMA, FW):
+        Y.dma_start(T.tab[:, a:a + FW], T.tab[:, 0:FW]).then_inc(T.sem.dfl, 16)
+    wait(Y, "ptsb", ("val", 8))
+    Y.dma_start(T.val[4:128:16, :], T.ptsb[:]).then_inc(T.sem.dvl, 16)
+    Y.wait_ge(T.sem.dvl, 16)
+    Y.dma_start(T.w3[:, 0:NE], T.val[:]).then_inc(T.sem.din, 16)
+    Y.dma_start(T.p1[:], T.val[:]).then_inc(T.sem.din, 16)
+    wait(Y, ("ga", 2), ("gb", 2))
+    Y.dma_start(T.xo[:], T.gat[4:128:16, :]).then_inc(T.sem.dxo, 16)
+    wait(Y, "ilo")
+    cuts0 = [NA] + list(range(CH * (NA // CH) + CH, HE + 1, CH))
+    pieces = ([(NA, QE)] if NA < QE else []) + [(max(NA, QE), HE)]
+    for h, cuts, nx in ((0, pieces, len(cuts0) - 1), (1, [(HE, HE + QE), (HE + QE, NE)], HE // CH)):
+        wait(Y, ("xc%d" % h, nx))
+        for a, b in cuts:
+            Y.dma_start(T.xx[2:128:16, a:b], T.ilo[0:8, a % CH:a % CH + b - a]).then_inc(T.sem["dx%d" % h], 16)
+    Y.wait_ge(T.sem.din, 32)
+    wait(Y, "scat", "cpre", "cap", "opre")
+    Y.wait_ge(T.sem.xa4, NEG // 2)
+    Y.dma_start(T.w3[2:128:16, 0:NE], T.xl4[:]).then_inc(T.sem.dr3, 16)
+    Y.wait_ge(T.sem.xa3, NEG // 2)
+    Y.dma_start(T.val[2:128:16, :], T.xl3[:]).then_inc(T.sem.dr2, 16)
+    Y.wait_ge(T.sem.xa2, NEG // 2)
+    Y.dma_start(T.p1[2:128:16, :], T.xl2[:]).then_inc(T.sem.dr1, 16)
+    wait(Y, "cs", ("xxi", 2), "tf")
+    for h in range(8):
+        Y.dma_start(T.xx[16 * h + 1:16 * h + 2, 0:NE], T.tf[:, 16 * h:16 * h + 16]).then_inc(T.sem.dnp, 16)
+    Y.wait_ge(T.sem.dpt, 16)
+    Y.dma_start(T.xx[2:128:16, 0:NE], T.ptf[:]).then_inc(T.sem.dnp, 16)
+
+    done(V.memset(T.tab[:, 0:FW], -BIG), "tab0")
+    wait(V, "pi")
+    done(V.tensor_scalar(T.pm[:], T.pi[:], 15, None, A.bitwise_and), "pm")
+    wait(V, "pm")
+    for k in (0, 3):
+        done(V.tensor_scalar(T["c%d" % k][:], T.pm[:], float(k), -1.0, A.is_equal, A.mult), "c%d" % k)
+    for k in (1, 2):
+        done(V.tensor_scalar(T["c%d" % k][:], T.pm[:], float(k), None, A.is_equal), "c%d" % k)
+    wait(V, "i8", "c0")
+    done(V.tensor_scalar(T.bcol[:], T.i8[:], T.c0[:], None, A.mult), "bcol")
+    wait(V, "lo", "c3", "bcol")
+    for a in range(8):
+        if a == 4:
+            V.wait_ge(T.sem.ldn, 16)
+            done(V.tensor_copy(T.nu[:], T.nxti[:]), "nu")
+        done(V.tensor_scalar(T.val[:, CH * a:CH * a + CH], T.lo[:], T.c3[:], T.bcol[:, a:a + 1], A.mult, A.add), "val")
+    V.wait_ge(T.sem.ldp, 16)
+    done(V.tensor_copy(T.ptsb[:], T.ptsi[:]), "ptsb")
+    V.wait_ge(T.sem.ldo, 16)
+    done(V.tensor_copy(T.ou[:], T.owni[:]), "ou")
+    done(V.memset(T.tab[:, FW:NVEC], -BIG), "tabv")
+    scuts = list(range(NVEC + NDMA + NGP, NV, FW)) + [NV]
+    wait(V, "ou", "tabv", "tabg", ("tabs", len(scuts) - 1), ("val", 8), "tab0")
+    V.wait_ge(T.sem.dvl, 16)
+    V.wait_ge(T.sem.dfl, 16 * (NDMA // FW))
+    done(V.tensor_copy(T.tab[:].indirect(T.ou[:, 0:128]), T.val[:]), "scat")
+    wait(V, "scat")
+    V.wait_ge(T.sem.narr, NEG)
+    done(V.tensor_copy(T.gat[:, 0:512], T.tab[:].indirect(T.nr[:, 0:32])), "ga")
+    done(V.tensor_copy(T.gat[:, 1024:1536], T.tab[:].indirect(T.nr[:, 64:96])), "gb")
+
+    wait(S, "tab0")
+    for a, b in zip(scuts, scuts[1:]):
+        done(S.activation(T.tab[:, a:b], T.tab[:, 0:b - a], F.Copy), "tabs")
+    wait(S, "c0", "c1", "c2", "c3", "i8")
+    done(S.activation(T.wc[:], T.c0[:], F.Identity, bias=T.c3[:], scale=float(CH)), "wc")
+    done(S.activation(T.c1n[:], T.c1[:], F.Copy, scale=-1.0), "cn")
+    done(S.activation(T.c2n[:], T.c2[:], F.Copy, scale=-1.0), "cn")
+    done(S.activation(T.bco1[:], T.i8[:], F.Identity, bias=SH, scale=T.c1[:]), "bco1")
+    wait(S, ("cn", 2))
+    done(S.activation(T.wi[:], T.c1n[:], F.Identity, bias=T.c2n[:], scale=float(CH)), "wc")
+    done(S.activation(T.bcn[:], T.i8[:], F.Copy, scale=T.c1n[:]), "bcn")
+    wait(S, "lo", "bcn")
+    ni = 0
+    for a in range(0, NA, CH):
+        b = min(a + CH, NA)
+        done(S.activation(T.ipat[:, a:b], T.lo[:, 0:b - a], F.Identity, bias=T.bcn[:, a // CH:a // CH + 1], scale=T.c2n[:]), "ipat")
+        ni += 1
+    wait(S, ("val", 8))
+    S.wait_ge(T.sem.dvl, 16)
+    done(S.activation(T.cwin[:, 0:CC], T.val[:, 0:CC], F.Silu, bias=SH + PF, scale=0.0), "cpre")
+    done(S.activation(T.ca[:, 0:CC], T.val[:, 0:CC], F.Identity, bias=-PF, scale=0.0), "cap")
+    wait(S, ("wc", 2), "bd", "z0")
+    done(S.activation(T.za[:, 15:143:16], T.bd[:, 0:128:16], F.Copy, scale=T.wc[:]), "za")
+    done(S.activation(T.owin[:, 0:ZZ], T.val[:, 0:ZZ], F.Identity, bias=T.c1n[:], scale=0.0), "opre")
+    wait(S, "ptsb")
+    done(S.activation(T.ptf[:], T.ptsb[:], F.Copy), "ptf")
+    wait(S, "scat")
+    S.wait_ge(T.sem.narr, NEG)
+    done(S.activation(T.gat[:, 512:1024], T.tab[:].indirect(T.nr[:, 32:64]), F.Copy), "ga")
+    done(S.activation(T.gat[:, 1536:2048], T.tab[:].indirect(T.nr[:, 96:128]), F.Copy), "gb")
+    wait(S, ("ga", 2), "bco1")
+    for h, cuts in ((0, cuts0), (1, list(range(HE, NE + 1, CH)))):
+        if h:
+            wait(S, ("gb", 2))
+        for a, b in zip(cuts, cuts[1:]):
+            done(S.activation(T.xx[:, a:b], T.gat[:, a:b], F.Identity, bias=T.bco1[:, a // CH:a // CH + 1], scale=-1.0), "xc%d" % h)
+    wait(S, ("z0", 3))
+    done(S.activation(T.zi[:, 15:143:16], T.bd[:, 0:128:16], F.Copy, scale=T.wi[:]), "zi")
+    done(S.activation(T.zk[:, 15:143:16], T.bd[:, 0:128:16], F.Copy, scale=T.c2[:]), "zk")
+    wait(S, "du", "cpre")
+    S.wait_ge(T.sem.dx0, 16 * len(pieces))
+    done(S.activation(T.cwin[:].indirect(T.du[:, NA // 16:64]), T.xx[:, NA:HE], F.Silu), "cs0")
+    wait(S, "cs0")
+    S.wait_ge(T.sem.dx1, 32)
+    done(S.activation(T.cwin[:].indirect(T.du[:, 64:128]), T.xx[:, HE:NE], F.Silu), "cs")
+    wait(S, "cs")
+    done(S.activation(T.cb[:], T.cwin[:, 0:CC], F.Identity, bias=SH + PF, scale=-1.0), "cb")
+    wait(S, "tr")
+    done(S.activation(T.tf[:], T.pst[:, 0:128], F.Copy), "tf")
+    wait(S, "pw")
+    done(S.activation(T.puf[:], T.psw[:, 0:32], F.Copy), "puf")
+    wait(S, "pq")
+    done(S.activation(T.icf[:], T.psi[:, 0:32], F.Copy), "icf")
+    wait(S, "pu", "b1", ("tails", 2))
+    done(S.activation(T.kk[:, HC:CC], T.b1[:].indirect(T.pu[:, HC // 16:CC // 16]), F.Sign, bias=0.5), "kk")
+    wait(S, "n1")
+    done(S.activation(T.rr[:, HC:CC], T.b1[:].indirect(T.pu[:, HC // 16:CC // 16]), F.Identity, scale=T.n1[:]), "rr")
+    wait(S, "ic")
+    S.wait_ge(T.sem.dnp, 16 * 9)
+    done(S.activation(T.cw[:], T.xx[:].indirect(T.ic[:, 0:32]), F.Copy), "cw")
+
+    def turn(ps, w, z, src, lo, hi, start, stop):
+        m = None
+        for s in range(16):
+            m = P.matmul(ps[:, 0:w], z[:, 15 - s:143 - s], src[:, lo + s:hi:16], start and s == 0, stop and s == 15)
+        return m
+
+    wait(P, "za")
+    for c, (ps, e, e2) in enumerate(((T.psf0, "fa", "ga"), (T.psf1, "fb", "gb"))):
+        wait(P, (e2, 2))
+        done(turn(ps, 64, T.za, T.gat, HE * c, HE * c + HE, True, True), e)
+    wait(P, "tri", "upp", ("vb", 2), ("vz", 2))
+    P.matmul(T.psd[:, 0:128], T.tri[:], T.vb[:, 1:129], True, False)
+    done(P.matmul(T.psd[:, 0:128], T.upp[:], T.vb[:, 0:128], False, True), "dl")
+    wait(P, "csa", ("iv", 2))
+    turn(T.psw, 32, T.za, T.ca, 0, CC, True, False)
+    wait(P, "zi")
+    turn(T.psi, 32, T.zi, T.ca, 0, CC, True, False)
+    wait(P, "ownf", "idf")
+    done(P.transpose(T.pst[:, 0:128], T.ownf[:], T.idf[:]), "tr")
+    wait(P, "cb")
+    done(turn(T.psw, 32, T.za, T.cb, 0, CC, False, True), "pw")
+    done(turn(T.psi, 32, T.zi, T.cb, 0, CC, False, True), "pq")
+    wait(P, "zk", ("kk", 2))
+    done(turn(T.psk, 32, T.zk, T.kk, 0, CC, True, True), "pk")
+    wait(P, "vb2", "du")
+    P.matmul(T.psd[:, 0:32], T.tri[:], T.vb2[:, 1:33], True, False)
+    done(P.matmul(T.psd[:, 0:32], T.upp[:], T.vb2[:, 0:32], False, True), "dl2")
+
+    done(V.tensor_copy(T.pmf[:], T.pm[:]), "pmf")
+    wait(V, "ii", "pmf", "c1")
+    done(V.tensor_scalar(T.i512[:], T.ii[:], T.pmf[:], None, A.add), "i512")
+    done(V.tensor_scalar(T.i128[:], T.ii[:, 0:32], T.pmf[:], float(ZZ - CC), A.add, A.add), "i128")
+    done(V.tensor_scalar(T.n1[:], T.c1[:], -1.0, 1.0, A.mult, A.add), "n1")
+    done(V.tensor_copy(T.ownf[:], T.owni[:]), "ownf")
+    wait(V, "i512")
+    for c, (ps, e) in enumerate(((T.psf0, "fa"), (T.psf1, "fb"))):
+        wait(V, e)
+        done(V.tensor_scalar(T.vb[:, 1 + 64 * c:65 + 64 * c], ps[:, 0:64], float(NE), None, A.is_lt), "vb")
+        done(V.tensor_scalar(T.fu[:, 64 * c:64 * c + 64], ps[:, 0:64], float(NONE), None, A.min), "fu")
+        done(V.tensor_scalar(T.psw[:, 64 * c:64 * c + 64], ps[:, 0:64], float(NE), None, A.is_ge), "nv")
+        wait(V, ("nv", c + 1))
+        done(V.tensor_tensor(T.iv[:, 64 * c:64 * c + 64], T.psw[:, 64 * c:64 * c + 64], T.i512[:, 64 * c:64 * c + 64], A.mult), "iv")
+    wait(V, "dl", "zf")
+    done(V.tensor_tensor_scan(T.psd[:, 128:256], T.psd[:, 0:128], T.zf[:], 0.0, A.add, A.add), "xs")
+    wait(V, "xs", ("iv", 2))
+    done(V.tensor_tensor(T.ds[:], T.psd[:, 128:256], T.iv[:], A.max), "ds")
+    wait(V, "ds")
+    done(V.tensor_copy(T.du[:], T.ds[:]), "du")
+    wait(V, "du", "cap", ("ipat", ni))
+    done(V.tensor_tensor(T.ca[:].indirect(T.du[:, 0:NA // 16]), T.gat[:, 0:NA], T.ipat[:], A.add), "csa")
+    V.wait_ge(T.sem.dr3, 16)
+    V.wait_ge(T.sem.dr2, 16)
+    wait(V, "w3t")
+    V.wait_ge(T.sem.fa2, NEG)
+    done(V.tensor_tensor(T.b2[:, 0:NE], T.w3[:].indirect(T.fl2[:, 0:128]), T.val[:], A.add), "b2")
+    V.wait_ge(T.sem.fa1, NEG)
+    V.wait_ge(T.sem.dr1, 16)
+    wait(V, ("tails", 2), "b2")
+    done(V.tensor_tensor(T.b1[:, 0:NE], T.b2[:].indirect(T.fl1[:, 0:128]), T.p1[:], A.add), "b1")
+    V.wait_ge(T.sem.qa1, NEG)
+    done(V.tensor_scalar(T.pu[:], T.pur[:], ROUND, ROUND, A.add, A.subtract), "pu")
+    wait(V, "pu", "b1")
+    done(V.tensor_scalar(T.kk[:, 0:HC], T.b1[:].indirect(T.pu[:, 0:HC // 16]), 0.0, None, A.is_ge), "kk")
+    wait(V, "n1")
+    done(V.tensor_scalar(T.rr[:, 0:HC], T.b1[:].indirect(T.pu[:, 0:HC // 16]), T.n1[:], None, A.mult), "rr")
+    V.wait_ge(T.sem.qa2, NEG)
+    done(V.tensor_scalar(T.ic[:], T.icr[:], ROUND, ROUND, A.add, A.subtract), "ic")
+    wait(V, "pk")
+    done(V.tensor_scalar(T.vb2[:, 1:33], T.psk[:, 0:32], 0.5, None, A.is_ge), "vb2")
+    done(V.tensor_scalar(T.nv2[:], T.psk[:, 0:32], 0.5, None, A.is_lt), "nv2")
+    wait(V, "nv2", "i128")
+    done(V.tensor_tensor(T.iv2[:], T.nv2[:], T.i128[:], A.mult), "iv2")
+    wait(V, "dl2")
+    done(V.tensor_tensor_scan(T.xs2[:], T.psd[:, 0:32], T.zf[:, 0:32], 0.0, A.add, A.add), "xs2")
+    wait(V, "xs2", "iv2")
+    done(V.tensor_tensor(T.ds2[:], T.xs2[:], T.iv2[:], A.max), "ds2")
+    wait(V, "ds2")
+    done(V.tensor_copy(T.du2[:], T.ds2[:]), "du2")
+    wait(V, "du2", ("rr", 2), "cw", "opre")
+    done(V.tensor_tensor(T.owin[:].indirect(T.du2[:, 0:32]), T.rr[:], T.cw[:], A.add), "osc")
+
+    wait(Y, "osc")
+    Y.dma_start(T.yk[:], T.owin[1:128:16, 0:ZZ]).then_inc(T.sem.out1, 16)
+    Y.wait_ge(T.sem.out1, 16)
+    wait(S, "osc")
+    S.dma_start(T.ys[:], T.owin[2:128:16, 0:ZZ]).then_inc(T.sem.out2, 16)
+    S.wait_ge(T.sem.out2, 16)
+    for s in ("nsent", "xsent", "fs2", "fs1", "qs1", "qs2"):
+        g.wait_ge(T.sem[s], 2 * NEG if s == "xsent" else NEG)

@@ -1,5 +1,4 @@
-from concourse.bass import DstId, RemoteDMATransfer
-from concourse.mybir import dt, AluOpType, AxisListType, ActivationFunctionType
+from concourse.mybir import AluOpType, ActivationFunctionType
 
 A = AluOpType
 F = ActivationFunctionType
@@ -7,20 +6,18 @@ NV = 16384
 NE = 2048
 HE = NE // 2
 QE = NE // 4
-CH = 256
-BIG = 8192.0
-PF = 8.0
-NONE = 8 * CH + 8
-DW = NONE + 8
-CC = 512
-HC = CC // 2
+BIG = 2048.0
+NONE = NE
+DW = NE + 16
 ZZ = 128
-SH = 16.0
-NA = 576
+ZW = 144
+FR = 1024.0
 NVEC = 6656
 NDMA = 4096
-NGP = 1024
+NGP = 1536
 FW = 1024
+X1 = 448
+KV = 4
 ROUND = 8388608.0
 
 
@@ -28,14 +25,14 @@ def _bufs():
     d = {}
     for where, typ, items in (
             ("sbuf", "int32", "owni:128 nxti:128 ptsi:128 pi:1 pm:1"),
-            ("sbuf", "uint16", "ou:128 nu:128 nr:128 fu:128 fl1:128 fl2:128 du:128 pu:32 ic:32 du2:32"),
-            ("sbuf", "bfloat16", "ptsb:128 xl1:128 p1:2048 w3:%d tab:16384 val:2048 gat:2048 lo:256 ipat:%d ca:%d cb:512 kk:512 ones:128"
-                                 " bd0:128 bd:128 tri:128 upp:128 za:144 zi:144 zk:144 vb:129 vb2:33" % (DW, NA, CC + NA)),
-            ("sbuf", "float32", "b2:%d b1:%d xx:%d ownf:128 ptf:128 tf:128 ilo:512 cwin:2560 rr:512 cw:512 owin:640"
-                                " zf:128 pmf:1 c0:1 c1:1 c2:1 c3:1 c1n:1 c2n:1 wc:1 wi:1 n1:1 i8:8 bcol:8 bco1:8 bcn:8 idf:128 onef:128"
-                                " ii:128 i512:128 i128:32 iv:128 ds:128 nv2:32 iv2:32 xs2:32 ds2:32 puf:32 icf:32 pur:32 icr:32" % (DW, DW, DW)),
-            ("dram", "bfloat16", "xo:128 xl2:128 xl3:128 xl4:128"),
-            ("psum", "float32", "psf0:512 psf1:512 psd:512 psw:512 psi:512 psk:512 pst:512")):
+            ("sbuf", "uint16", "ou:128 nu:128 nr:128 fu:128 fl0:128 fl2:128 yu:128 yl:128 cu:8"),
+            ("sbuf", "bfloat16", "ptsb:128 pl3:128 hi:128 lo:128 tab:16384 val:%d gat:%d yy:2048 xx:%d zz:2048 zw:%d ones:128 bd0:128 bd:128"
+                                 " up0:128 upp:128 vb:128 tt:128 cmp:%d rst:%d sc:%d junk:%d" % (DW, DW, DW, 3 * ZW, 128 * KV, 128 * KV, 128 * KV, 128 * (8 - KV))),
+            ("sbuf", "float16", "bdh:8 ssel:128"),
+            ("sbuf", "float32", "v0:128 v1:128 w0:128 w1:128 ws:128 wr:128 wd:128 nm:136 key:136 sa:136 zf:128 pmf:1 i16:8 mh:8 one8:8 bd1:8 bdf:8"
+                                " acc:8 mrow:128 sel:128 nsel:128 ok:128 osum:128"),
+            ("dram", "bfloat16", "xo:128 xl:128"),
+            ("psum", "float32", "pa:512 pb:512 pza:512 pzb:512 pc:512 pu:512 pk:512 ps:512")):
         for it in items.split():
             name, w = it.split(":")
             d[name] = (where, [128, int(w)], typ)
@@ -43,11 +40,10 @@ def _bufs():
 
 
 SCRATCH = _bufs()
-EV = """ones tabg tab0 tabv tabs pi pm pmf c0 c1 c2 c3 cn n1 wc lo ilo i8 bcol bco1 bcn val onef bd0 bd tri upp idf zf z0 za zi zk ipat cap xxi
-ii i512 i128 w3t tails cpre vz opre ownf ptf tr tf ptsb nu ou scat ga gb fa fb fu vb nv iv dl xs ds du
-xc0 xc1 csa cs0 cs cb pw pq puf icf pu ic kk pk b2 b1 rr cw vb2 nv2 iv2 dl2 xs2 ds2 du2 osc""".split()
-SEMAPHORES = ["e_" + e for e in EV] + ["ldo", "ldn", "ldp", "dfl", "dvl", "din", "dxo", "dnp", "dx0", "dx1", "dr1", "dr2", "dr3", "dpt", "narr", "nsent",
-                                       "xa1", "xa2", "xa3", "xa4", "xsent", "fa1", "fa2", "fs1", "fs2", "qa1", "qa2", "qs1", "qs2", "out1", "out2"]
+EV = """hi lo tab0 val0 tabv tabg tabs ptsb ou nu scat sc i8 zs za zz zp p0 pi i16 bd1 bdf bd0 bd up0 upp mrow ga gb fa fb pm pmf mh nm bdh fu v0
+ya yb ta tb yu v1 xx za1 zb1 qa qb ws wr wd vb sa cnt pu tt cmp key sc2 acc cu sel nsel ssel pk ps ok osum rst0""".split()
+SEMAPHORES = ["e_" + e for e in EV] + ["ldo", "ldn", "ldp", "dfl", "dvl", "dxo", "dr5", "dr6", "narr", "parr", "fa0", "fb0", "f2r", "xar", "v0r",
+                                       "yar", "ybr", "v1r", "sent", "out1", "out2"]
 
 
 def rank_program(g, core, T, topo):
@@ -56,8 +52,9 @@ def rank_program(g, core, T, topo):
         return
     n = len(T.cores)
     V, S, P, Y = g.vector, g.scalar, g.tensor, g.sync
-    back = [T.cores[(rank - k) % n] for k in range(n)]
-    after = T.cores[(rank + 1) % n]
+    at = lambda k: T.cores[(rank + k) % n]
+    za, zz, zp = (T.zw[:, ZW * k:ZW * k + ZW] for k in range(3))
+    zcol = lambda k: T.zw[:, ZW * k + 15:ZW * k + 143:16]
 
     def sem(e):
         return T.sem["e_" + e]
@@ -72,286 +69,269 @@ def rank_program(g, core, T, topo):
             else:
                 q.wait_ge(sem(e), 1)
 
-    def const(buf, v, e):
-        done(g.iota(buf, [[0, buf.shape[1]]], int(v), 0, allow_small_or_imprecise_dtypes=True), e)
-
-    es = set(topo.engines(core, after))
-    for k in range(1, n - 1):
-        es &= set(topo.engines(core, back[k]))
+    es = set(topo.engines(core, at(1)))
+    for k in range(2, n):
+        es &= set(topo.engines(core, at(k)))
     E = sorted(es)[0:8]
     M = sum(1 << e for e in E)
     NEG = len(E)
+    sends = [0]
 
-    def send(dst_ap, src_ap, dst, rs, ls):
-        rid, pid = topo.addr(dst)[:2]
-        g.remote_dma(dst_ap, src_ap, T.sem[rs], T.sem[ls], pid, rid, M)
+    def send(dst_ap, src_ap, k, rs):
+        rid, pid = topo.addr(at(k))[:2]
+        g.remote_dma(dst_ap, src_ap, T.sem[rs], T.sem.sent, pid, rid, M)
+        sends[0] += 1
 
-    def send_x(k1, k2):
-        tr = []
-        for k, half in ((k1, E[:NEG // 2]), (k2, E[NEG // 2:])):
-            rid, pid = topo.addr(back[k])[:2]
-            tr.append(RemoteDMATransfer(dst_ids=[DstId(rid=rid, pnc=pid)], dma_engine_mask=sum(1 << e for e in half), remote_sem=T.sem["xa%d" % k],
-                                        srcs=[T.xo[:]], dsts=[T["xl%d" % k][:]]))
-        g.remote_dma_fused(tr, local_sem=T.sem.xsent)
+    def iota(buf, pat, base, cm, e):
+        done(g.iota(buf, pat, base, cm, allow_small_or_imprecise_dtypes=True), e)
 
-    Y.dma_start(T.owni[:], T.own[:]).then_inc(T.sem.ldo, 16)
-    S.dma_start(T.nxti[:], T.nxt[:]).then_inc(T.sem.ldn, 16)
     Y.dma_start(T.ptsi[:], T.pts[:]).then_inc(T.sem.ldp, 16)
+    S.dma_start(T.nxti[:], T.nxt[:]).then_inc(T.sem.ldn, 16)
+    Y.dma_start(T.owni[:], T.own[:]).then_inc(T.sem.ldo, 16)
 
-    done(g.iota(T.pi[:], [[0, 1]], 0, 1), "pi")
-    done(g.iota(T.i8[:], [[1, 8]], 0, 0, allow_small_or_imprecise_dtypes=True), "i8")
-    done(g.iota(T.lo[:], [[1, CH]], 0, 0, allow_small_or_imprecise_dtypes=True), "lo")
-    const(T.tab[:, NVEC + NDMA:NVEC + NDMA + NGP], -BIG, "tabg")
+    iota(T.hi[:], [[0, 128]], 0, -1, "hi")
+    iota(T.lo[:], [[-1, 128]], 0, 0, "lo")
+    iota(T.tab[:, NVEC + NDMA:NVEC + NDMA + NGP], [[0, NGP]], -int(BIG), 0, "tabg")
     wait(g, "nu")
-    send(T.nr[:], T.nu[:], after, "narr", "nsent")
-    const(T.ones[:], 1, "ones")
-    wait(g, "ones")
+    send(T.nr[:], T.nu[:], 1, "narr")
+    wait(g, "ptsb")
+    send(T.pl3[:], T.ptsb[:], -3, "parr")
+    done(g.iota(T.pi[:], [[0, 1]], 0, 1), "pi")
+    iota(T.i16[:], [[16, 8]], 0, 0, "i16")
+    wait(g, ("zs", 2))
+
+    def weight(k, row, w, e, cnt):
+        if cnt:
+            wait(g, (e, cnt))
+        done(g.affine_select(zcol(k), zcol(k), [[-16, 8]], A.not_equal, w, -row, 1), e)
+
+    weight(2, 4, 1 / FR, "zp", 0)
+    iota(zcol(0), [[1, 8]], 0, 0, "i8")
+    weight(1, 5, 1 / FR, "zz", 0)
+    wait(g, "i8")
+    done(g.affine_select(zcol(0), zcol(0), [[-16, 8]], A.is_equal, 0.0, -1, 1), "za")
+    weight(1, 6, 1 / FR, "zz", 1)
+    weight(0, 0, -128.0, "za", 1)
+    done(g.affine_select(T.bd1[:], T.one8[:], [[-16, 8]], A.is_ge, 0.0, 0, 1), "bd1")
+    weight(0, 3, -1.0, "za", 2)
+    wait(g, "bd1")
+    done(g.affine_select(T.bdf[:], T.bd1[:], [[16, 8]], A.is_ge, 0.0, 15, -1), "bdf")
+    weight(0, 4, 1 / FR, "za", 3)
+    wait(g, "fu")
+    send(T.fl0[:, 0:64], T.fu[:, 0:64], 1, "fa0")
+    wait(g, ("fu", 2))
+    send(T.fl0[:, 64:128], T.fu[:, 64:128], 1, "fb0")
+    g.wait_ge(T.sem.dxo, 16)
+    send(T.xl[:], T.xo[:], -4, "xar")
+    send(T.fl2[:], T.fu[:], -3, "f2r")
+    wait(g, ("v0", 2))
+    send(T.w0[:], T.v0[:], -1, "v0r")
+    wait(g, "sc")
     done(g.affine_select(T.bd0[:], T.ones[:], [[-16, 8], [0, 16]], A.is_ge, 0.0, 0, 1), "bd0")
     wait(g, "bd0")
     done(g.affine_select(T.bd[:], T.bd0[:], [[16, 8], [0, 16]], A.is_ge, 0.0, 15, -1), "bd")
-    const(T.za[:], 0, "z0")
+    wait(g, "yu")
+    send(T.yl[:, 0:64], T.yu[:, 0:64], -2, "yar")
+    wait(g, ("yu", 2))
+    send(T.yl[:, 64:128], T.yu[:, 64:128], -2, "ybr")
+    wait(g, ("v1", 2))
+    send(T.w1[:], T.v1[:], -2, "v1r")
     wait(g, "bd")
-    done(g.affine_select(T.tri[:], T.bd[:], [[1, 128]], A.is_gt, 0.0, 0, -1), "tri")
-    done(g.affine_select(T.upp[:], T.bd[:], [[-1, 128]], A.is_ge, 0.0, 0, 1), "upp")
-    done(g.iota(T.ii[:], [[16, 128]], CC, 0, allow_small_or_imprecise_dtypes=True), "ii")
-    const(T.zf[:], 0, "zf")
-    const(T.vb[:, 0:1], 0, "vz")
-    const(T.vb2[:, 0:1], 0, "vz")
-    done(g.iota(T.ilo[0:8, :], [[0, QE // CH], [1, CH]], int(SH), 0, allow_small_or_imprecise_dtypes=True), "ilo")
-    wait(g, "za")
-    const(T.zi[:], 0, "z0")
-    const(T.zk[:], 0, "z0")
-    const(T.w3[:, NE:DW], -BIG, "w3t")
-    g.wait_ge(T.sem.dxo, 16)
-    send_x(4, 3)
-    wait(g, ("fu", 2))
-    send(T.fl2[:], T.fu[:], back[3], "fa2", "fs2")
-    send(T.fl1[:], T.fu[:], back[2], "fa1", "fs1")
-    send_x(2, 1)
-    for b in ("b2", "b1"):
-        const(T[b][:, NE:DW], -BIG, "tails")
-    const(T.onef[:], 1, "onef")
-    wait(g, "onef")
-    done(g.affine_select(T.idf[:], T.onef[:], [[-1, 128]], A.is_equal, 0.0, 0, 1), "idf")
-    const(T.xx[:, 0:NA], 0, "xxi")
-    const(T.xx[:, NE:DW], 0, "xxi")
-    wait(g, "ptf")
-    g.wait_ge(T.sem.xa1, NEG // 2)
-    g.dma_start(T.ptf[:], T.xl1[:], accum_op=A.add).then_inc(T.sem.dpt, 16)
-    wait(g, "puf")
-    send(T.pur[:], T.puf[:], back[1], "qa1", "qs1")
-    wait(g, "icf")
-    send(T.icr[:], T.icf[:], back[1], "qa2", "qs2")
+    done(g.affine_select(T.up0[:], T.bd[:], [[-1, 128]], A.is_ge, 0.0, 0, 1), "up0")
+    iota(T.mrow[:], [[1, 128]], 256, 0, "mrow")
+    wait(g, "up0")
+    done(g.affine_select(T.upp[:], T.up0[:], [[-1, 128]], A.not_equal, -255.0, 0, 1), "upp")
+
+    fills = list(range(NVEC, NVEC + NDMA, FW))
+
+    def fill(cols):
+        for a in cols:
+            Y.dma_start(T.tab[:, a:a + FW], T.tab[:, 0:FW]).then_inc(T.sem.dfl, 16)
 
     wait(Y, "tab0")
-    for a in range(NVEC, NVEC + NDMA, FW):
-        Y.dma_start(T.tab[:, a:a + FW], T.tab[:, 0:FW]).then_inc(T.sem.dfl, 16)
-    wait(Y, "ptsb", ("val", 8))
-    Y.dma_start(T.val[4:128:16, :], T.ptsb[:]).then_inc(T.sem.dvl, 16)
-    Y.wait_ge(T.sem.dvl, 16)
-    Y.dma_start(T.w3[:, 0:NE], T.val[:]).then_inc(T.sem.din, 16)
-    Y.dma_start(T.p1[:], T.val[:]).then_inc(T.sem.din, 16)
+    fill(fills[:2])
+    wait(Y, "val0", "hi", "lo")
+    Y.dma_start(T.val[0:128:16, 0:NE], T.hi[:]).then_inc(T.sem.dvl, 16)
+    Y.dma_start(T.val[3:128:16, 0:NE], T.lo[:]).then_inc(T.sem.dvl, 16)
+    wait(Y, "ptsb")
+    Y.dma_start(T.val[4:128:16, 0:NE], T.ptsb[:]).then_inc(T.sem.dvl, 16)
+    fill(fills[2:])
+    wait(Y, "scat", "p0", "sc")
+    Y.wait_ge(T.sem.parr, NEG)
+    Y.dma_start(T.val[5:128:16, 0:NE], T.pl3[:]).then_inc(T.sem.dr5, 16)
     wait(Y, ("ga", 2), ("gb", 2))
-    Y.dma_start(T.xo[:], T.gat[4:128:16, :]).then_inc(T.sem.dxo, 16)
-    wait(Y, "ilo")
-    cuts0 = [NA] + list(range(CH * (NA // CH) + CH, HE + 1, CH))
-    pieces = ([(NA, QE)] if NA < QE else []) + [(max(NA, QE), HE)]
-    for h, cuts, nx in ((0, pieces, len(cuts0) - 1), (1, [(HE, HE + QE), (HE + QE, NE)], HE // CH)):
-        wait(Y, ("xc%d" % h, nx))
-        for a, b in cuts:
-            Y.dma_start(T.xx[2:128:16, a:b], T.ilo[0:8, a % CH:a % CH + b - a]).then_inc(T.sem["dx%d" % h], 16)
-    Y.wait_ge(T.sem.din, 32)
-    wait(Y, "scat", "cpre", "cap", "opre")
-    Y.wait_ge(T.sem.xa4, NEG // 2)
-    Y.dma_start(T.w3[2:128:16, 0:NE], T.xl4[:]).then_inc(T.sem.dr3, 16)
-    Y.wait_ge(T.sem.xa3, NEG // 2)
-    Y.dma_start(T.val[2:128:16, :], T.xl3[:]).then_inc(T.sem.dr2, 16)
-    Y.wait_ge(T.sem.xa2, NEG // 2)
-    Y.dma_start(T.p1[2:128:16, :], T.xl2[:]).then_inc(T.sem.dr1, 16)
-    wait(Y, "cs", ("xxi", 2), "tf")
-    for h in range(8):
-        Y.dma_start(T.xx[16 * h + 1:16 * h + 2, 0:NE], T.tf[:, 16 * h:16 * h + 16]).then_inc(T.sem.dnp, 16)
-    Y.wait_ge(T.sem.dpt, 16)
-    Y.dma_start(T.xx[2:128:16, 0:NE], T.ptf[:]).then_inc(T.sem.dnp, 16)
+    Y.dma_start(T.xo[:], T.gat[4:128:16, 0:NE]).then_inc(T.sem.dxo, 16)
+    Y.wait_ge(T.sem.xar, NEG)
+    Y.dma_start(T.val[6:128:16, 0:NE], T.xl[:]).then_inc(T.sem.dr6, 16)
+
+    def vgather(out, win, off, a, b, e):
+        done(V.tensor_copy(out[:, a:b], win[:].indirect(off[:, a // 16:b // 16])), e)
+
+    def sgather(out, win, off, a, b, e):
+        done(S.activation(out[:, a:b], win[:].indirect(off[:, a // 16:b // 16]), F.Copy), e)
 
     done(V.memset(T.tab[:, 0:FW], -BIG), "tab0")
-    wait(V, "pi")
-    done(V.tensor_scalar(T.pm[:], T.pi[:], 15, None, A.bitwise_and), "pm")
-    wait(V, "pm")
-    for k in (0, 3):
-        done(V.tensor_scalar(T["c%d" % k][:], T.pm[:], float(k), -1.0, A.is_equal, A.mult), "c%d" % k)
-    for k in (1, 2):
-        done(V.tensor_scalar(T["c%d" % k][:], T.pm[:], float(k), None, A.is_equal), "c%d" % k)
-    wait(V, "i8", "c0")
-    done(V.tensor_scalar(T.bcol[:], T.i8[:], T.c0[:], None, A.mult), "bcol")
-    wait(V, "lo", "c3", "bcol")
-    for a in range(8):
-        if a == 4:
-            V.wait_ge(T.sem.ldn, 16)
-            done(V.tensor_copy(T.nu[:], T.nxti[:]), "nu")
-        done(V.tensor_scalar(T.val[:, CH * a:CH * a + CH], T.lo[:], T.c3[:], T.bcol[:, a:a + 1], A.mult, A.add), "val")
+    done(V.memset(T.val[:], -BIG), "val0")
+    done(V.memset(T.tab[:, FW:2 * FW], -BIG), "tabv")
     V.wait_ge(T.sem.ldp, 16)
     done(V.tensor_copy(T.ptsb[:], T.ptsi[:]), "ptsb")
+    V.wait_ge(T.sem.ldn, 16)
+    done(V.tensor_copy(T.nu[:], T.nxti[:]), "nu")
     V.wait_ge(T.sem.ldo, 16)
     done(V.tensor_copy(T.ou[:], T.owni[:]), "ou")
-    done(V.memset(T.tab[:, FW:NVEC], -BIG), "tabv")
+    done(V.memset(T.tab[:, 2 * FW:NVEC], -BIG), "tabv")
     scuts = list(range(NVEC + NDMA + NGP, NV, FW)) + [NV]
-    wait(V, "ou", "tabv", "tabg", ("tabs", len(scuts) - 1), ("val", 8), "tab0")
-    V.wait_ge(T.sem.dvl, 16)
-    V.wait_ge(T.sem.dfl, 16 * (NDMA // FW))
-    done(V.tensor_copy(T.tab[:].indirect(T.ou[:, 0:128]), T.val[:]), "scat")
+    wait(V, "ou", ("tabv", 2), "tabg", ("tabs", len(scuts) - 1), "val0", "tab0")
+    V.wait_ge(T.sem.dvl, 48)
+    V.wait_ge(T.sem.dfl, 16 * len(fills))
+    done(V.tensor_copy(T.tab[:].indirect(T.ou[:, 0:128]), T.val[:, 0:NE]), "scat")
     wait(V, "scat")
     V.wait_ge(T.sem.narr, NEG)
-    done(V.tensor_copy(T.gat[:, 0:512], T.tab[:].indirect(T.nr[:, 0:32])), "ga")
-    done(V.tensor_copy(T.gat[:, 1024:1536], T.tab[:].indirect(T.nr[:, 64:96])), "gb")
+    vgather(T.gat, T.tab, T.nr, 0, QE, "ga")
+    vgather(T.gat, T.tab, T.nr, HE, HE + QE, "gb")
+    wait(V, "pi", "sc")
+    done(V.tensor_scalar(T.pm[:], T.pi[:], 15, None, A.bitwise_and), "pm")
+    done(V.tensor_scalar(T.nm[:, 0:128], T.owni[:], 1.0, None, A.add), "nm")
+    for c, (ps, e) in enumerate(((T.pa, "fa"), (T.pb, "fb"))):
+        wait(V, e)
+        done(V.tensor_scalar(T.fu[:, 64 * c:64 * c + 64], ps[:, 0:64], float(NONE), None, A.min), "fu")
+        done(V.tensor_copy(T.v0[:, 64 * c:64 * c + 64], ps[:, 0:64]), "v0")
+        if c == 0:
+            wait(V, "pm", "i16", "bdf")
+            done(V.tensor_copy(T.pmf[:], T.pm[:]), "pmf")
+            done(V.tensor_copy(T.bdh[:], T.bdf[:]), "bdh")
+            wait(V, "pmf")
+            done(V.tensor_scalar(T.mh[:], T.i16[:], T.pmf[:], 0.5, A.add, A.add), "mh")
+    wait(V, ("ga", 2), ("gb", 2))
+    V.wait_ge(T.sem.fa0, NEG)
+    vgather(T.yy, T.gat, T.fl0, 0, QE, "ya")
+    V.wait_ge(T.sem.fb0, NEG)
+    vgather(T.yy, T.gat, T.fl0, HE, HE + QE, "yb")
+    wait(V, "ta")
+    done(V.tensor_scalar(T.yu[:, 0:64], T.pa[:, 0:64], float(NONE), None, A.min), "yu")
+    V.wait_ge(T.sem.f2r, NEG)
+    V.wait_ge(T.sem.dr5, 16)
+    V.wait_ge(T.sem.dr6, 16)
+    vgather(T.xx, T.val, T.fl2, 0, X1, "xx")
+    wait(V, "tb")
+    done(V.tensor_scalar(T.yu[:, 64:128], T.pb[:, 0:64], float(NONE), None, A.min), "yu")
+    vgather(T.xx, T.val, T.fl2, X1, HE, "xx")
+    wait(V, ("xx", 3))
+    V.wait_ge(T.sem.yar, NEG)
+    vgather(T.zz, T.xx, T.yl, 0, QE, "za1")
+    V.wait_ge(T.sem.ybr, NEG)
+    vgather(T.zz, T.xx, T.yl, HE, HE + QE, "zb1")
+    V.wait_ge(T.sem.v0r, NEG)
+    V.wait_ge(T.sem.v1r, NEG)
+    done(V.tensor_tensor(T.ws[:], T.w0[:], T.w1[:], A.add), "ws")
+    wait(V, "qa")
+    done(V.tensor_scalar(T.vb[:, 0:64], T.pza[:, 0:64], 0.0, None, A.is_ge), "vb")
+    wait(V, "ws")
+    done(V.tensor_scalar(T.wr[:], T.ws[:], ROUND, ROUND, A.add, A.subtract), "wr")
+    wait(V, "wr")
+    done(V.tensor_tensor(T.wd[:], T.ws[:], T.wr[:], A.subtract), "wd")
+    wait(V, "wd")
+    done(V.tensor_tensor(T.sa[:, 0:64], T.pza[:, 0:64], T.wd[:, 0:64], A.add), "sa")
+    wait(V, "qb")
+    done(V.tensor_scalar(T.vb[:, 64:128], T.pzb[:, 0:64], 0.0, None, A.is_ge), "vb")
+    done(V.tensor_tensor(T.sa[:, 64:128], T.pzb[:, 0:64], T.wd[:, 64:128], A.add), "sa")
+    wait(V, "cnt")
+    done(V.tensor_tensor_scan(T.tt[:], T.pc[:, 0:128], T.zf[:], 0.0, A.add, A.add), "tt")
+    wait(V, "tt", "mh")
+    for k in range(KV):
+        done(V.tensor_scalar(T.cmp[:, 128 * k:128 * k + 128], T.tt[:], T.mh[:, k:k + 1], None, A.is_le), "cmp")
+    wait(V, "pu")
+    done(V.tensor_tensor(T.key[:, 0:128], T.tt[:], T.pu[:, 0:128], A.subtract), "key")
+    wait(V, ("cmp", KV))
+    done(V.tensor_tensor_scan(T.sc[:], T.rst[:], T.cmp[:], 0.0, A.mult, A.add), "sc2")
+    wait(V, "sc2")
+    done(V.tensor_scalar(T.cu[:, 0:KV], T.sc[:, 127:128 * KV:128], 0.0, None, A.add), "cu")
+    wait(V, ("acc", 8 - KV))
+    done(V.tensor_scalar(T.cu[:, KV:8], T.acc[:, KV:8], 0.5, 64.0, A.mult, A.add), "cu")
+    wait(V, ("cu", 2), "key", "mrow")
+    done(V.tensor_tensor(T.sel[:], T.key[:].indirect(T.cu[:, 0:8]), T.mrow[:], A.is_equal), "sel")
+    wait(V, "sel", "nm", ("sa", 2))
+    done(V.tensor_tensor(T.nsel[:], T.nm[:].indirect(T.cu[:, 0:8]), T.sel[:], A.mult), "nsel")
+    done(V.tensor_tensor(T.ssel[:], T.sa[:].indirect(T.cu[:, 0:8]), T.sel[:], A.mult), "ssel")
+    wait(V, "ps")
+    done(V.tensor_scalar(T.osum[0:8, :], T.ps[0:8, 0:ZZ], FR, None, A.mult), "osum")
 
     wait(S, "tab0")
     for a, b in zip(scuts, scuts[1:]):
         done(S.activation(T.tab[:, a:b], T.tab[:, 0:b - a], F.Copy), "tabs")
-    wait(S, "c0", "c1", "c2", "c3", "i8")
-    done(S.activation(T.wc[:], T.c0[:], F.Identity, bias=T.c3[:], scale=float(CH)), "wc")
-    done(S.activation(T.c1n[:], T.c1[:], F.Copy, scale=-1.0), "cn")
-    done(S.activation(T.c2n[:], T.c2[:], F.Copy, scale=-1.0), "cn")
-    done(S.activation(T.bco1[:], T.i8[:], F.Identity, bias=SH, scale=T.c1[:]), "bco1")
-    wait(S, ("cn", 2))
-    done(S.activation(T.wi[:], T.c1n[:], F.Identity, bias=T.c2n[:], scale=float(CH)), "wc")
-    done(S.activation(T.bcn[:], T.i8[:], F.Copy, scale=T.c1n[:]), "bcn")
-    wait(S, "lo", "bcn")
-    ni = 0
-    for a in range(0, NA, CH):
-        b = min(a + CH, NA)
-        done(S.activation(T.ipat[:, a:b], T.lo[:, 0:b - a], F.Identity, bias=T.bcn[:, a // CH:a // CH + 1], scale=T.c2n[:]), "ipat")
-        ni += 1
-    wait(S, ("val", 8))
-    S.wait_ge(T.sem.dvl, 16)
-    done(S.activation(T.cwin[:, 0:CC], T.val[:, 0:CC], F.Silu, bias=SH + PF, scale=0.0), "cpre")
-    done(S.activation(T.ca[:, 0:CC], T.val[:, 0:CC], F.Identity, bias=-PF, scale=0.0), "cap")
-    wait(S, ("wc", 2), "bd", "z0")
-    done(S.activation(T.za[:, 15:143:16], T.bd[:, 0:128:16], F.Copy, scale=T.wc[:]), "za")
-    done(S.activation(T.owin[:, 0:ZZ], T.val[:, 0:ZZ], F.Identity, bias=T.c1n[:], scale=0.0), "opre")
-    wait(S, "ptsb")
-    done(S.activation(T.ptf[:], T.ptsb[:], F.Copy), "ptf")
-    wait(S, "scat")
-    S.wait_ge(T.sem.narr, NEG)
-    done(S.activation(T.gat[:, 512:1024], T.tab[:].indirect(T.nr[:, 32:64]), F.Copy), "ga")
-    done(S.activation(T.gat[:, 1536:2048], T.tab[:].indirect(T.nr[:, 96:128]), F.Copy), "gb")
-    wait(S, ("ga", 2), "bco1")
-    for h, cuts in ((0, cuts0), (1, list(range(HE, NE + 1, CH)))):
-        if h:
-            wait(S, ("gb", 2))
-        for a, b in zip(cuts, cuts[1:]):
-            done(S.activation(T.xx[:, a:b], T.gat[:, a:b], F.Identity, bias=T.bco1[:, a // CH:a // CH + 1], scale=-1.0), "xc%d" % h)
-    wait(S, ("z0", 3))
-    done(S.activation(T.zi[:, 15:143:16], T.bd[:, 0:128:16], F.Copy, scale=T.wi[:]), "zi")
-    done(S.activation(T.zk[:, 15:143:16], T.bd[:, 0:128:16], F.Copy, scale=T.c2[:]), "zk")
-    wait(S, "du", "cpre")
-    S.wait_ge(T.sem.dx0, 16 * len(pieces))
-    done(S.activation(T.cwin[:].indirect(T.du[:, NA // 16:64]), T.xx[:, NA:HE], F.Silu), "cs0")
-    wait(S, "cs0")
-    S.wait_ge(T.sem.dx1, 32)
-    done(S.activation(T.cwin[:].indirect(T.du[:, 64:128]), T.xx[:, HE:NE], F.Silu), "cs")
-    wait(S, "cs")
-    done(S.activation(T.cb[:], T.cwin[:, 0:CC], F.Identity, bias=SH + PF, scale=-1.0), "cb")
-    wait(S, "tr")
-    done(S.activation(T.tf[:], T.pst[:, 0:128], F.Copy), "tf")
-    wait(S, "pw")
-    done(S.activation(T.puf[:], T.psw[:, 0:32], F.Copy), "puf")
-    wait(S, "pq")
-    done(S.activation(T.icf[:], T.psi[:, 0:32], F.Copy), "icf")
-    wait(S, "pu", "b1", ("tails", 2))
-    done(S.activation(T.kk[:, HC:CC], T.b1[:].indirect(T.pu[:, HC // 16:CC // 16]), F.Sign, bias=0.5), "kk")
-    wait(S, "n1")
-    done(S.activation(T.rr[:, HC:CC], T.b1[:].indirect(T.pu[:, HC // 16:CC // 16]), F.Identity, scale=T.n1[:]), "rr")
-    wait(S, "ic")
-    S.wait_ge(T.sem.dnp, 16 * 9)
-    done(S.activation(T.cw[:], T.xx[:].indirect(T.ic[:, 0:32]), F.Copy), "cw")
+    S.wait_ge(T.sem.dvl, 48)
 
-    def turn(ps, w, z, src, lo, hi, start, stop):
+    def const(buf, v):
+        return S.activation(buf, T.val[:, 0:buf.shape[1]], F.Identity, bias=v, scale=0.0)
+
+    done(const(T.one8[:], 1.0), "zs")
+    done(const(T.zw[:], 0.0), "zs")
+    rest = [(T.rst[:], 1.0), (T.ones[:], 1.0), (T.gat[:, NE:DW], -BIG), (T.xx[:, NE:DW], -BIG), (T.zf[:], 0.0),
+            (T.nm[:, 128:136], 0.0), (T.key[:, 128:136], 0.0), (T.sa[:, 128:136], 0.0)]
+    for buf, v in rest:
+        done(const(buf, v), "rst0")
+    wait(S, ("rst0", len(rest)))
+    done(S.activation(T.rst[:, 0:128 * KV:128], T.val[:, 0:KV], F.Copy, scale=0.0), "sc")
+    wait(S, "scat", "sc")
+    S.wait_ge(T.sem.narr, NEG)
+    sgather(T.gat, T.tab, T.nr, QE, HE, "ga")
+    sgather(T.gat, T.tab, T.nr, HE + QE, NE, "gb")
+    wait(S, ("ga", 2), ("gb", 2))
+    S.wait_ge(T.sem.fa0, NEG)
+    sgather(T.yy, T.gat, T.fl0, QE, HE, "ya")
+    S.wait_ge(T.sem.fb0, NEG)
+    sgather(T.yy, T.gat, T.fl0, HE + QE, NE, "yb")
+    S.wait_ge(T.sem.f2r, NEG)
+    S.wait_ge(T.sem.dr5, 16)
+    S.wait_ge(T.sem.dr6, 16)
+    sgather(T.xx, T.val, T.fl2, HE, NE, "xx")
+    for c, ps in enumerate((T.pa, T.pb)):
+        wait(S, ("yu", c + 1))
+        done(S.activation(T.v1[:, 64 * c:64 * c + 64], ps[:, 0:64], F.Copy), "v1")
+    wait(S, ("xx", 3))
+    S.wait_ge(T.sem.yar, NEG)
+    sgather(T.zz, T.xx, T.yl, QE, HE, "za1")
+    S.wait_ge(T.sem.ybr, NEG)
+    sgather(T.zz, T.xx, T.yl, HE + QE, NE, "zb1")
+    wait(S, "tt", "mh")
+    for k in range(KV, 8):
+        done(S.activation(T.junk[:, 128 * (k - KV):128 * (k - KV) + 128], T.tt[:], F.Sign, bias=T.mh[:, k:k + 1], scale=-1.0,
+                          accum_out=T.acc[:, k:k + 1]), "acc")
+    wait(S, "pk")
+    done(S.activation(T.ok[0:8, :], T.pk[0:8, 0:ZZ], F.Identity, bias=-1.0), "ok")
+
+    def turn(ps, z, src, c, start, stop):
         m = None
         for s in range(16):
-            m = P.matmul(ps[:, 0:w], z[:, 15 - s:143 - s], src[:, lo + s:hi:16], start and s == 0, stop and s == 15)
+            m = P.matmul(ps[:, 0:64], z[:, 15 - s:143 - s], src[:, HE * c + s:HE * c + HE:16], start and s == 0, stop and s == 15)
         return m
 
-    wait(P, "za")
-    for c, (ps, e, e2) in enumerate(((T.psf0, "fa", "ga"), (T.psf1, "fb", "gb"))):
+    wait(P, "zp")
+    P.wait_ge(T.sem.dvl, 48)
+    turn(T.pza, zp, T.val, 0, True, False)
+    done(turn(T.pzb, zp, T.val, 1, True, False), "p0")
+    wait(P, ("za", 4), ("zz", 2))
+    for c, (ps, e, e2) in enumerate(((T.pa, "fa", "ga"), (T.pb, "fb", "gb"))):
         wait(P, (e2, 2))
-        done(turn(ps, 64, T.za, T.gat, HE * c, HE * c + HE, True, True), e)
-    wait(P, "tri", "upp", ("vb", 2), ("vz", 2))
-    P.matmul(T.psd[:, 0:128], T.tri[:], T.vb[:, 1:129], True, False)
-    done(P.matmul(T.psd[:, 0:128], T.upp[:], T.vb[:, 0:128], False, True), "dl")
-    wait(P, "csa", ("iv", 2))
-    turn(T.psw, 32, T.za, T.ca, 0, CC, True, False)
-    wait(P, "zi")
-    turn(T.psi, 32, T.zi, T.ca, 0, CC, True, False)
-    wait(P, "ownf", "idf")
-    done(P.transpose(T.pst[:, 0:128], T.ownf[:], T.idf[:]), "tr")
-    wait(P, "cb")
-    done(turn(T.psw, 32, T.za, T.cb, 0, CC, False, True), "pw")
-    done(turn(T.psi, 32, T.zi, T.cb, 0, CC, False, True), "pq")
-    wait(P, "zk", ("kk", 2))
-    done(turn(T.psk, 32, T.zk, T.kk, 0, CC, True, True), "pk")
-    wait(P, "vb2", "du")
-    P.matmul(T.psd[:, 0:32], T.tri[:], T.vb2[:, 1:33], True, False)
-    done(P.matmul(T.psd[:, 0:32], T.upp[:], T.vb2[:, 0:32], False, True), "dl2")
+        done(turn(ps, za, T.gat, c, True, True), e)
+    for c, (ps, e, e2) in enumerate(((T.pa, "ta", "ya"), (T.pb, "tb", "yb"))):
+        wait(P, (e2, 2), ("fu", c + 1), ("v0", c + 1))
+        done(turn(ps, za, T.yy, c, True, True), e)
+    for c, (ps, e, e2) in enumerate(((T.pza, "qa", "za1"), (T.pzb, "qb", "zb1"))):
+        wait(P, (e2, 2))
+        done(turn(ps, zz, T.zz, c, False, True), e)
+    wait(P, ("vb", 2), "bd", "upp")
+    done(P.matmul(T.pc[:, 0:128], T.bd[:], T.vb[:], True, True), "cnt")
+    done(P.matmul(T.pu[:, 0:128], T.upp[:], T.vb[:], True, True), "pu")
+    wait(P, "nsel")
+    done(P.matmul(T.pk[0:8, 0:ZZ], T.bdf[:], T.nsel[:], True, True), "pk")
+    wait(P, "ssel", "bdh")
+    done(P.matmul(T.ps[0:8, 0:ZZ], T.bdh[:], T.ssel[:], True, True), "ps")
 
-    done(V.tensor_copy(T.pmf[:], T.pm[:]), "pmf")
-    wait(V, "ii", "pmf", "c1")
-    done(V.tensor_scalar(T.i512[:], T.ii[:], T.pmf[:], None, A.add), "i512")
-    done(V.tensor_scalar(T.i128[:], T.ii[:, 0:32], T.pmf[:], float(ZZ - CC), A.add, A.add), "i128")
-    done(V.tensor_scalar(T.n1[:], T.c1[:], -1.0, 1.0, A.mult, A.add), "n1")
-    done(V.tensor_copy(T.ownf[:], T.owni[:]), "ownf")
-    wait(V, "i512")
-    for c, (ps, e) in enumerate(((T.psf0, "fa"), (T.psf1, "fb"))):
-        wait(V, e)
-        done(V.tensor_scalar(T.vb[:, 1 + 64 * c:65 + 64 * c], ps[:, 0:64], float(NE), None, A.is_lt), "vb")
-        done(V.tensor_scalar(T.fu[:, 64 * c:64 * c + 64], ps[:, 0:64], float(NONE), None, A.min), "fu")
-        done(V.tensor_scalar(T.psw[:, 64 * c:64 * c + 64], ps[:, 0:64], float(NE), None, A.is_ge), "nv")
-        wait(V, ("nv", c + 1))
-        done(V.tensor_tensor(T.iv[:, 64 * c:64 * c + 64], T.psw[:, 64 * c:64 * c + 64], T.i512[:, 64 * c:64 * c + 64], A.mult), "iv")
-    wait(V, "dl", "zf")
-    done(V.tensor_tensor_scan(T.psd[:, 128:256], T.psd[:, 0:128], T.zf[:], 0.0, A.add, A.add), "xs")
-    wait(V, "xs", ("iv", 2))
-    done(V.tensor_tensor(T.ds[:], T.psd[:, 128:256], T.iv[:], A.max), "ds")
-    wait(V, "ds")
-    done(V.tensor_copy(T.du[:], T.ds[:]), "du")
-    wait(V, "du", "cap", ("ipat", ni))
-    done(V.tensor_tensor(T.ca[:].indirect(T.du[:, 0:NA // 16]), T.gat[:, 0:NA], T.ipat[:], A.add), "csa")
-    V.wait_ge(T.sem.dr3, 16)
-    V.wait_ge(T.sem.dr2, 16)
-    wait(V, "w3t")
-    V.wait_ge(T.sem.fa2, NEG)
-    done(V.tensor_tensor(T.b2[:, 0:NE], T.w3[:].indirect(T.fl2[:, 0:128]), T.val[:], A.add), "b2")
-    V.wait_ge(T.sem.fa1, NEG)
-    V.wait_ge(T.sem.dr1, 16)
-    wait(V, ("tails", 2), "b2")
-    done(V.tensor_tensor(T.b1[:, 0:NE], T.b2[:].indirect(T.fl1[:, 0:128]), T.p1[:], A.add), "b1")
-    V.wait_ge(T.sem.qa1, NEG)
-    done(V.tensor_scalar(T.pu[:], T.pur[:], ROUND, ROUND, A.add, A.subtract), "pu")
-    wait(V, "pu", "b1")
-    done(V.tensor_scalar(T.kk[:, 0:HC], T.b1[:].indirect(T.pu[:, 0:HC // 16]), 0.0, None, A.is_ge), "kk")
-    wait(V, "n1")
-    done(V.tensor_scalar(T.rr[:, 0:HC], T.b1[:].indirect(T.pu[:, 0:HC // 16]), T.n1[:], None, A.mult), "rr")
-    V.wait_ge(T.sem.qa2, NEG)
-    done(V.tensor_scalar(T.ic[:], T.icr[:], ROUND, ROUND, A.add, A.subtract), "ic")
-    wait(V, "pk")
-    done(V.tensor_scalar(T.vb2[:, 1:33], T.psk[:, 0:32], 0.5, None, A.is_ge), "vb2")
-    done(V.tensor_scalar(T.nv2[:], T.psk[:, 0:32], 0.5, None, A.is_lt), "nv2")
-    wait(V, "nv2", "i128")
-    done(V.tensor_tensor(T.iv2[:], T.nv2[:], T.i128[:], A.mult), "iv2")
-    wait(V, "dl2")
-    done(V.tensor_tensor_scan(T.xs2[:], T.psd[:, 0:32], T.zf[:, 0:32], 0.0, A.add, A.add), "xs2")
-    wait(V, "xs2", "iv2")
-    done(V.tensor_tensor(T.ds2[:], T.xs2[:], T.iv2[:], A.max), "ds2")
-    wait(V, "ds2")
-    done(V.tensor_copy(T.du2[:], T.ds2[:]), "du2")
-    wait(V, "du2", ("rr", 2), "cw", "opre")
-    done(V.tensor_tensor(T.owin[:].indirect(T.du2[:, 0:32]), T.rr[:], T.cw[:], A.add), "osc")
-
-    wait(Y, "osc")
-    Y.dma_start(T.yk[:], T.owin[1:128:16, 0:ZZ]).then_inc(T.sem.out1, 16)
-    Y.wait_ge(T.sem.out1, 16)
-    wait(S, "osc")
-    S.dma_start(T.ys[:], T.owin[2:128:16, 0:ZZ]).then_inc(T.sem.out2, 16)
-    S.wait_ge(T.sem.out2, 16)
-    for s in ("nsent", "xsent", "fs2", "fs1", "qs1", "qs2"):
-        g.wait_ge(T.sem[s], 2 * NEG if s == "xsent" else NEG)
+    wait(S, "ok")
+    S.dma_start(T.yk[:], T.ok[0:8, :]).then_inc(T.sem.out1, 16)
+    S.wait_ge(T.sem.out1, 16)
+    wait(Y, "osum")
+    Y.dma_start(T.ys[:], T.osum[0:8, :]).then_inc(T.sem.out2, 16)
+    Y.wait_ge(T.sem.out2, 16)
+    g.wait_ge(T.sem.sent, NEG * sends[0])

from concourse.mybir import AluOpType, ActivationFunctionType

A = AluOpType
F = ActivationFunctionType
NV = 16384
NE = 2048
HE = NE // 2
QE = NE // 4
BIG = 2048.0
NONE = NE
DW = NE + 16
ZZ = 128
ZW = 144
FR = 1024.0
NVEC = 6656
NDMA = 4096
NGP = 1536
FW = 1024
X1 = 448
KV = 4
ROUND = 8388608.0


def _bufs():
    d = {}
    for where, typ, items in (
            ("sbuf", "int32", "owni:128 nxti:128 ptsi:128 pi:1 pm:1"),
            ("sbuf", "uint16", "ou:128 nu:128 nr:128 fu:128 fl0:128 fl2:128 yu:128 yl:128 cu:8"),
            ("sbuf", "bfloat16", "ptsb:128 pl3:128 hi:128 lo:128 tab:16384 val:%d gat:%d yy:2048 xx:%d zz:2048 zw:%d ones:128 bd0:128 bd:128"
                                 " up0:128 upp:128 vb:128 tt:128 cmp:%d rst:%d sc:%d junk:%d" % (DW, DW, DW, 3 * ZW, 128 * KV, 128 * KV, 128 * KV, 128 * (8 - KV))),
            ("sbuf", "float16", "bdh:8 ssel:128"),
            ("sbuf", "float32", "v0:128 v1:128 w0:128 w1:128 ws:128 wr:128 wd:128 nm:136 key:136 sa:136 zf:128 pmf:1 i16:8 mh:8 one8:8 bd1:8 bdf:8"
                                " acc:8 mrow:128 sel:128 nsel:128 ok:128 osum:128"),
            ("dram", "bfloat16", "xo:128 xl:128"),
            ("psum", "float32", "pa:512 pb:512 pza:512 pzb:512 pc:512 pu:512 pk:512 ps:512")):
        for it in items.split():
            name, w = it.split(":")
            d[name] = (where, [128, int(w)], typ)
    return d


SCRATCH = _bufs()
EV = """hi lo tab0 val0 tabv tabg tabs ptsb ou nu scat sc i8 zs za zz zp p0 pi i16 bd1 bdf bd0 bd up0 upp mrow ga gb fa fb pm pmf mh nm bdh fu v0
ya yb ta tb yu v1 xx za1 zb1 qa qb ws wr wd vb sa cnt pu tt cmp key sc2 acc cu sel nsel ssel pk ps ok osum rst0""".split()
SEMAPHORES = ["e_" + e for e in EV] + ["ldo", "ldn", "ldp", "dfl", "dvl", "dxo", "dr5", "dr6", "narr", "parr", "fa0", "fb0", "f2r", "xar", "v0r",
                                       "yar", "ybr", "v1r", "sent", "out1", "out2"]


def rank_program(g, core, T, topo):
    rank = T.rank_of(core)
    if rank is None:
        return
    n = len(T.cores)
    V, S, P, Y = g.vector, g.scalar, g.tensor, g.sync
    at = lambda k: T.cores[(rank + k) % n]
    za, zz, zp = (T.zw[:, ZW * k:ZW * k + ZW] for k in range(3))
    zcol = lambda k: T.zw[:, ZW * k + 15:ZW * k + 143:16]

    def sem(e):
        return T.sem["e_" + e]

    def done(ins, e):
        ins.then_inc(sem(e), 1)

    def wait(q, *es):
        for e in es:
            if isinstance(e, tuple):
                q.wait_ge(sem(e[0]), e[1])
            else:
                q.wait_ge(sem(e), 1)

    es = set(topo.engines(core, at(1)))
    for k in range(2, n):
        es &= set(topo.engines(core, at(k)))
    E = sorted(es)[0:8]
    M = sum(1 << e for e in E)
    NEG = len(E)
    sends = [0]

    def send(dst_ap, src_ap, k, rs):
        rid, pid = topo.addr(at(k))[:2]
        g.remote_dma(dst_ap, src_ap, T.sem[rs], T.sem.sent, pid, rid, M)
        sends[0] += 1

    def iota(buf, pat, base, cm, e):
        done(g.iota(buf, pat, base, cm, allow_small_or_imprecise_dtypes=True), e)

    Y.dma_start(T.ptsi[:], T.pts[:]).then_inc(T.sem.ldp, 16)
    S.dma_start(T.nxti[:], T.nxt[:]).then_inc(T.sem.ldn, 16)
    Y.dma_start(T.owni[:], T.own[:]).then_inc(T.sem.ldo, 16)

    iota(T.hi[:], [[0, 128]], 0, -1, "hi")
    iota(T.lo[:], [[-1, 128]], 0, 0, "lo")
    iota(T.tab[:, NVEC + NDMA:NVEC + NDMA + NGP], [[0, NGP]], -int(BIG), 0, "tabg")
    wait(g, "nu")
    send(T.nr[:], T.nu[:], 1, "narr")
    wait(g, "ptsb")
    send(T.pl3[:], T.ptsb[:], -3, "parr")
    done(g.iota(T.pi[:], [[0, 1]], 0, 1), "pi")
    iota(T.i16[:], [[16, 8]], 0, 0, "i16")
    wait(g, ("zs", 2))

    def weight(k, row, w, e, cnt):
        if cnt:
            wait(g, (e, cnt))
        done(g.affine_select(zcol(k), zcol(k), [[-16, 8]], A.not_equal, w, -row, 1), e)

    weight(2, 4, 1 / FR, "zp", 0)
    iota(zcol(0), [[1, 8]], 0, 0, "i8")
    weight(1, 5, 1 / FR, "zz", 0)
    wait(g, "i8")
    done(g.affine_select(zcol(0), zcol(0), [[-16, 8]], A.is_equal, 0.0, -1, 1), "za")
    weight(1, 6, 1 / FR, "zz", 1)
    weight(0, 0, -128.0, "za", 1)
    done(g.affine_select(T.bd1[:], T.one8[:], [[-16, 8]], A.is_ge, 0.0, 0, 1), "bd1")
    weight(0, 3, -1.0, "za", 2)
    wait(g, "bd1")
    done(g.affine_select(T.bdf[:], T.bd1[:], [[16, 8]], A.is_ge, 0.0, 15, -1), "bdf")
    weight(0, 4, 1 / FR, "za", 3)
    wait(g, "fu")
    send(T.fl0[:, 0:64], T.fu[:, 0:64], 1, "fa0")
    wait(g, ("fu", 2))
    send(T.fl0[:, 64:128], T.fu[:, 64:128], 1, "fb0")
    g.wait_ge(T.sem.dxo, 16)
    send(T.xl[:], T.xo[:], -4, "xar")
    send(T.fl2[:], T.fu[:], -3, "f2r")
    wait(g, ("v0", 2))
    send(T.w0[:], T.v0[:], -1, "v0r")
    wait(g, "sc")
    done(g.affine_select(T.bd0[:], T.ones[:], [[-16, 8], [0, 16]], A.is_ge, 0.0, 0, 1), "bd0")
    wait(g, "bd0")
    done(g.affine_select(T.bd[:], T.bd0[:], [[16, 8], [0, 16]], A.is_ge, 0.0, 15, -1), "bd")
    wait(g, "yu")
    send(T.yl[:, 0:64], T.yu[:, 0:64], -2, "yar")
    wait(g, ("yu", 2))
    send(T.yl[:, 64:128], T.yu[:, 64:128], -2, "ybr")
    wait(g, ("v1", 2))
    send(T.w1[:], T.v1[:], -2, "v1r")
    wait(g, "bd")
    done(g.affine_select(T.up0[:], T.bd[:], [[-1, 128]], A.is_ge, 0.0, 0, 1), "up0")
    iota(T.mrow[:], [[1, 128]], 256, 0, "mrow")
    wait(g, "up0")
    done(g.affine_select(T.upp[:], T.up0[:], [[-1, 128]], A.not_equal, -255.0, 0, 1), "upp")

    fills = list(range(NVEC, NVEC + NDMA, FW))

    def fill(cols):
        for a in cols:
            Y.dma_start(T.tab[:, a:a + FW], T.tab[:, 0:FW]).then_inc(T.sem.dfl, 16)

    wait(Y, "tab0")
    fill(fills[:2])
    wait(Y, "val0", "hi", "lo")
    Y.dma_start(T.val[0:128:16, 0:NE], T.hi[:]).then_inc(T.sem.dvl, 16)
    Y.dma_start(T.val[3:128:16, 0:NE], T.lo[:]).then_inc(T.sem.dvl, 16)
    wait(Y, "ptsb")
    Y.dma_start(T.val[4:128:16, 0:NE], T.ptsb[:]).then_inc(T.sem.dvl, 16)
    fill(fills[2:])
    wait(Y, "scat", "p0", "sc")
    Y.wait_ge(T.sem.parr, NEG)
    Y.dma_start(T.val[5:128:16, 0:NE], T.pl3[:]).then_inc(T.sem.dr5, 16)
    wait(Y, ("ga", 2), ("gb", 2))
    Y.dma_start(T.xo[:], T.gat[4:128:16, 0:NE]).then_inc(T.sem.dxo, 16)
    Y.wait_ge(T.sem.xar, NEG)
    Y.dma_start(T.val[6:128:16, 0:NE], T.xl[:]).then_inc(T.sem.dr6, 16)

    def vgather(out, win, off, a, b, e):
        done(V.tensor_copy(out[:, a:b], win[:].indirect(off[:, a // 16:b // 16])), e)

    def sgather(out, win, off, a, b, e):
        done(S.activation(out[:, a:b], win[:].indirect(off[:, a // 16:b // 16]), F.Copy), e)

    done(V.memset(T.tab[:, 0:FW], -BIG), "tab0")
    done(V.memset(T.val[:], -BIG), "val0")
    done(V.memset(T.tab[:, FW:2 * FW], -BIG), "tabv")
    V.wait_ge(T.sem.ldp, 16)
    done(V.tensor_copy(T.ptsb[:], T.ptsi[:]), "ptsb")
    V.wait_ge(T.sem.ldn, 16)
    done(V.tensor_copy(T.nu[:], T.nxti[:]), "nu")
    V.wait_ge(T.sem.ldo, 16)
    done(V.tensor_copy(T.ou[:], T.owni[:]), "ou")
    done(V.memset(T.tab[:, 2 * FW:NVEC], -BIG), "tabv")
    scuts = list(range(NVEC + NDMA + NGP, NV, FW)) + [NV]
    wait(V, "ou", ("tabv", 2), "tabg", ("tabs", len(scuts) - 1), "val0", "tab0")
    V.wait_ge(T.sem.dvl, 48)
    V.wait_ge(T.sem.dfl, 16 * len(fills))
    done(V.tensor_copy(T.tab[:].indirect(T.ou[:, 0:128]), T.val[:, 0:NE]), "scat")
    wait(V, "scat")
    V.wait_ge(T.sem.narr, NEG)
    vgather(T.gat, T.tab, T.nr, 0, QE, "ga")
    vgather(T.gat, T.tab, T.nr, HE, HE + QE, "gb")
    wait(V, "pi", "sc")
    done(V.tensor_scalar(T.pm[:], T.pi[:], 15, None, A.bitwise_and), "pm")
    done(V.tensor_scalar(T.nm[:, 0:128], T.owni[:], 1.0, None, A.add), "nm")
    for c, (ps, e) in enumerate(((T.pa, "fa"), (T.pb, "fb"))):
        wait(V, e)
        done(V.tensor_scalar(T.fu[:, 64 * c:64 * c + 64], ps[:, 0:64], float(NONE), None, A.min), "fu")
        done(V.tensor_copy(T.v0[:, 64 * c:64 * c + 64], ps[:, 0:64]), "v0")
        if c == 0:
            wait(V, "pm", "i16", "bdf")
            done(V.tensor_copy(T.pmf[:], T.pm[:]), "pmf")
            done(V.tensor_copy(T.bdh[:], T.bdf[:]), "bdh")
            wait(V, "pmf")
            done(V.tensor_scalar(T.mh[:], T.i16[:], T.pmf[:], 0.5, A.add, A.add), "mh")
    wait(V, ("ga", 2), ("gb", 2))
    V.wait_ge(T.sem.fa0, NEG)
    vgather(T.yy, T.gat, T.fl0, 0, QE, "ya")
    V.wait_ge(T.sem.fb0, NEG)
    vgather(T.yy, T.gat, T.fl0, HE, HE + QE, "yb")
    wait(V, "ta")
    done(V.tensor_scalar(T.yu[:, 0:64], T.pa[:, 0:64], float(NONE), None, A.min), "yu")
    V.wait_ge(T.sem.f2r, NEG)
    V.wait_ge(T.sem.dr5, 16)
    V.wait_ge(T.sem.dr6, 16)
    vgather(T.xx, T.val, T.fl2, 0, X1, "xx")
    wait(V, "tb")
    done(V.tensor_scalar(T.yu[:, 64:128], T.pb[:, 0:64], float(NONE), None, A.min), "yu")
    vgather(T.xx, T.val, T.fl2, X1, HE, "xx")
    wait(V, ("xx", 3))
    V.wait_ge(T.sem.yar, NEG)
    vgather(T.zz, T.xx, T.yl, 0, QE, "za1")
    V.wait_ge(T.sem.ybr, NEG)
    vgather(T.zz, T.xx, T.yl, HE, HE + QE, "zb1")
    V.wait_ge(T.sem.v0r, NEG)
    V.wait_ge(T.sem.v1r, NEG)
    done(V.tensor_tensor(T.ws[:], T.w0[:], T.w1[:], A.add), "ws")
    wait(V, "qa")
    done(V.tensor_scalar(T.vb[:, 0:64], T.pza[:, 0:64], 0.0, None, A.is_ge), "vb")
    wait(V, "ws")
    done(V.tensor_scalar(T.wr[:], T.ws[:], ROUND, ROUND, A.add, A.subtract), "wr")
    wait(V, "wr")
    done(V.tensor_tensor(T.wd[:], T.ws[:], T.wr[:], A.subtract), "wd")
    wait(V, "wd")
    done(V.tensor_tensor(T.sa[:, 0:64], T.pza[:, 0:64], T.wd[:, 0:64], A.add), "sa")
    wait(V, "qb")
    done(V.tensor_scalar(T.vb[:, 64:128], T.pzb[:, 0:64], 0.0, None, A.is_ge), "vb")
    done(V.tensor_tensor(T.sa[:, 64:128], T.pzb[:, 0:64], T.wd[:, 64:128], A.add), "sa")
    wait(V, "cnt")
    done(V.tensor_tensor_scan(T.tt[:], T.pc[:, 0:128], T.zf[:], 0.0, A.add, A.add), "tt")
    wait(V, "tt", "mh")
    for k in range(KV):
        done(V.tensor_scalar(T.cmp[:, 128 * k:128 * k + 128], T.tt[:], T.mh[:, k:k + 1], None, A.is_le), "cmp")
    wait(V, "pu")
    done(V.tensor_tensor(T.key[:, 0:128], T.tt[:], T.pu[:, 0:128], A.subtract), "key")
    wait(V, ("cmp", KV))
    done(V.tensor_tensor_scan(T.sc[:], T.rst[:], T.cmp[:], 0.0, A.mult, A.add), "sc2")
    wait(V, "sc2")
    done(V.tensor_scalar(T.cu[:, 0:KV], T.sc[:, 127:128 * KV:128], 0.0, None, A.add), "cu")
    wait(V, ("acc", 8 - KV))
    done(V.tensor_scalar(T.cu[:, KV:8], T.acc[:, KV:8], 0.5, 64.0, A.mult, A.add), "cu")
    wait(V, ("cu", 2), "key", "mrow")
    done(V.tensor_tensor(T.sel[:], T.key[:].indirect(T.cu[:, 0:8]), T.mrow[:], A.is_equal), "sel")
    wait(V, "sel", "nm", ("sa", 2))
    done(V.tensor_tensor(T.nsel[:], T.nm[:].indirect(T.cu[:, 0:8]), T.sel[:], A.mult), "nsel")
    done(V.tensor_tensor(T.ssel[:], T.sa[:].indirect(T.cu[:, 0:8]), T.sel[:], A.mult), "ssel")
    wait(V, "ps")
    done(V.tensor_scalar(T.osum[0:8, :], T.ps[0:8, 0:ZZ], FR, None, A.mult), "osum")

    wait(S, "tab0")
    for a, b in zip(scuts, scuts[1:]):
        done(S.activation(T.tab[:, a:b], T.tab[:, 0:b - a], F.Copy), "tabs")
    S.wait_ge(T.sem.dvl, 48)

    def const(buf, v):
        return S.activation(buf, T.val[:, 0:buf.shape[1]], F.Identity, bias=v, scale=0.0)

    done(const(T.one8[:], 1.0), "zs")
    done(const(T.zw[:], 0.0), "zs")
    rest = [(T.rst[:], 1.0), (T.ones[:], 1.0), (T.gat[:, NE:DW], -BIG), (T.xx[:, NE:DW], -BIG), (T.zf[:], 0.0),
            (T.nm[:, 128:136], 0.0), (T.key[:, 128:136], 0.0), (T.sa[:, 128:136], 0.0)]
    for buf, v in rest:
        done(const(buf, v), "rst0")
    wait(S, ("rst0", len(rest)))
    done(S.activation(T.rst[:, 0:128 * KV:128], T.val[:, 0:KV], F.Copy, scale=0.0), "sc")
    wait(S, "scat", "sc")
    S.wait_ge(T.sem.narr, NEG)
    sgather(T.gat, T.tab, T.nr, QE, HE, "ga")
    sgather(T.gat, T.tab, T.nr, HE + QE, NE, "gb")
    wait(S, ("ga", 2), ("gb", 2))
    S.wait_ge(T.sem.fa0, NEG)
    sgather(T.yy, T.gat, T.fl0, QE, HE, "ya")
    S.wait_ge(T.sem.fb0, NEG)
    sgather(T.yy, T.gat, T.fl0, HE + QE, NE, "yb")
    S.wait_ge(T.sem.f2r, NEG)
    S.wait_ge(T.sem.dr5, 16)
    S.wait_ge(T.sem.dr6, 16)
    sgather(T.xx, T.val, T.fl2, HE, NE, "xx")
    for c, ps in enumerate((T.pa, T.pb)):
        wait(S, ("yu", c + 1))
        done(S.activation(T.v1[:, 64 * c:64 * c + 64], ps[:, 0:64], F.Copy), "v1")
    wait(S, ("xx", 3))
    S.wait_ge(T.sem.yar, NEG)
    sgather(T.zz, T.xx, T.yl, QE, HE, "za1")
    S.wait_ge(T.sem.ybr, NEG)
    sgather(T.zz, T.xx, T.yl, HE + QE, NE, "zb1")
    wait(S, "tt", "mh")
    for k in range(KV, 8):
        done(S.activation(T.junk[:, 128 * (k - KV):128 * (k - KV) + 128], T.tt[:], F.Sign, bias=T.mh[:, k:k + 1], scale=-1.0,
                          accum_out=T.acc[:, k:k + 1]), "acc")
    wait(S, "pk")
    done(S.activation(T.ok[0:8, :], T.pk[0:8, 0:ZZ], F.Identity, bias=-1.0), "ok")

    def turn(ps, z, src, c, start, stop):
        m = None
        for s in range(16):
            m = P.matmul(ps[:, 0:64], z[:, 15 - s:143 - s], src[:, HE * c + s:HE * c + HE:16], start and s == 0, stop and s == 15)
        return m

    wait(P, "zp")
    P.wait_ge(T.sem.dvl, 48)
    turn(T.pza, zp, T.val, 0, True, False)
    done(turn(T.pzb, zp, T.val, 1, True, False), "p0")
    wait(P, ("za", 4), ("zz", 2))
    for c, (ps, e, e2) in enumerate(((T.pa, "fa", "ga"), (T.pb, "fb", "gb"))):
        wait(P, (e2, 2))
        done(turn(ps, za, T.gat, c, True, True), e)
    for c, (ps, e, e2) in enumerate(((T.pa, "ta", "ya"), (T.pb, "tb", "yb"))):
        wait(P, (e2, 2), ("fu", c + 1), ("v0", c + 1))
        done(turn(ps, za, T.yy, c, True, True), e)
    for c, (ps, e, e2) in enumerate(((T.pza, "qa", "za1"), (T.pzb, "qb", "zb1"))):
        wait(P, (e2, 2))
        done(turn(ps, zz, T.zz, c, False, True), e)
    wait(P, ("vb", 2), "bd", "upp")
    done(P.matmul(T.pc[:, 0:128], T.bd[:], T.vb[:], True, True), "cnt")
    done(P.matmul(T.pu[:, 0:128], T.upp[:], T.vb[:], True, True), "pu")
    wait(P, "nsel")
    done(P.matmul(T.pk[0:8, 0:ZZ], T.bdf[:], T.nsel[:], True, True), "pk")
    wait(P, "ssel", "bdh")
    done(P.matmul(T.ps[0:8, 0:ZZ], T.bdh[:], T.ssel[:], True, True), "ps")

    wait(S, "ok")
    S.dma_start(T.yk[:], T.ok[0:8, :]).then_inc(T.sem.out1, 16)
    S.wait_ge(T.sem.out1, 16)
    wait(Y, "osum")
    Y.dma_start(T.ys[:], T.osum[0:8, :]).then_inc(T.sem.out2, 16)
    Y.wait_ge(T.sem.out2, 16)
    g.wait_ge(T.sem.sent, NEG * sends[0])
